import numpy as np, ml_dtypes
CORES = [66,74,82,90,194,202,210,218]
N = 8
import mx_ref
BF = ml_dtypes.bfloat16
def gcols(t, e):
    v = np.concatenate([t.reshape(8, 16, -1, 4), np.zeros((8, 16, 1, 4), BF)], axis=2)
    return np.ascontiguousarray(np.stack([v[g][:, e[g]] for g in range(8)])).reshape(128, -1)
def tile(rs):
    return np.stack(rs, axis=2).reshape(128, -1).astype(BF)
def pick(q, e):
    c = np.concatenate([q[0].reshape(128, -1, 4), np.zeros((128, 1, 4), np.uint8)], axis=1); s = np.concatenate([q[1], np.ones((16, 1), np.uint8)], axis=1)
    return (np.ascontiguousarray(c[:, e].reshape(128, -1)), np.ascontiguousarray(s[:, e]))
def join(*qs):
    return (np.concatenate([q[0] for q in qs], axis=1), np.concatenate([q[1] for q in qs], axis=1))
def put(q, e, v):
    c, s = q[0].reshape(128, -1, 4).copy(), q[1].copy(); c[:, e] = v[0].reshape(128, -1, 4); s[:, e] = v[1]
    return (c.reshape(128, -1), s)
def pk(c, s):
    return (np.ascontiguousarray(c), mx_ref.live(s))
def emit(q):
    return q[0], q[1]
def packed(v, rng):
    q = [mx_ref.quantize(np.ascontiguousarray(v[r])) for r in range(N)]
    return np.stack([a for a, b in q]), np.stack([mx_ref.plane(b, rng) for a, b in q])
def values_of_codes():
    e, c = np.zeros((128, 128, 4), np.float32), np.zeros((128, 2, 4), np.uint8)
    e[np.arange(128), np.arange(128), 0] = 1
    c[:127, :, 0] = np.arange(256).reshape(2, 128).T[:127]
    return mx_ref.matmul(mx_ref.quantize(e.reshape(128, 512).astype(BF)), (c.reshape(128, 8), np.full((16, 2), 127, np.uint8))).T.reshape(-1).astype(np.float64)
CODE_VALUE, SCALE_VALUE = values_of_codes(), 2.0 ** (np.arange(256) - 127.0)
def decode(q):
    return (CODE_VALUE[q[0]].reshape(16, 8, -1, 4) * SCALE_VALUE[q[1]][:, None, :, None] + 0.0).reshape(128, -1).astype(np.float32)
def f(rng, *shape):
    return mx_ref.flush((rng.standard_normal(shape, dtype=np.float32) * np.exp2(rng.integers(-2, 3, shape[:-1] + (1,)))).astype(BF))
def wide(rng, *shape, cols=0):
    v = rng.standard_normal(shape, dtype=np.float32) * np.exp2(rng.integers(-12, 13, shape)).astype(np.float32)
    if cols: v *= np.repeat(np.exp2(rng.integers(-cols, cols + 1, shape[:-2] + (1, shape[-1] // 4))) * (rng.random(shape[:-2] + (1, shape[-1] // 4)) > 0.0625), 4, axis=-1).astype(np.float32)
    return mx_ref.flush(v.astype(BF))
C, V, R = 352, 17, 3
STEP = [1, 2, 4]
def match(a, b):
    k = (np.arange(C)[:, None] + np.arange(-V, V + 1)) % C
    return np.argmin(np.abs(a[:, :, None] - b[:, k]), axis=2) - V
def inherit(d, e):
    place = np.arange(C)
    ok = np.take_along_axis(e, (place + d) % C, axis=1) == -d
    before = np.maximum.accumulate(np.where(ok, place, -1), axis=1)
    behind = np.minimum.accumulate(np.where(ok, place, C)[:, ::-1], axis=1)[:, ::-1]
    before, behind = np.where(before < 0, behind, before), np.where(behind == C, before, behind)
    z = np.concatenate([d, np.zeros((8, 1), int)], axis=1)
    return np.take_along_axis(z, before, axis=1), np.take_along_axis(z, behind, axis=1)
def big(v):
    v = v.astype(np.float32)
    v[np.abs(v) < np.float32(2.0 ** -16)] = 0
    return v.astype(BF)
def numbers_of(rng):
    return {"x": big(f(rng, N, 128, 4 * C)), "u": np.array(f(rng, N, 128, 512)), "v": np.array(f(rng, N, 128, 512))}
def weights(rng, still=[]):
    w = np.array(f(rng, N, 128, 2048)).reshape(N, 8, 16, 4, 8, 16, 4)
    for i in still:
        w[:, :, i] = 0
        w[:, :, :, :, :, i] = 0
    c, p = packed(w.reshape(N, 128, 2048), rng)
    return {"wc": c, "ws": p}
def digits(k, n):
    z = k[..., None] & (1 << np.arange(4 * n))
    return np.stack([z[..., 4 * i:4 * i + 4] for i in range(n)], axis=2)
def signs(rng):
    p = rng.permutation(8)
    m = (p // 2) ^ (p % 2 * (N - 1))
    c = np.array([[1.0 - 2 * (bin(r & int(k)).count("1") % 2) for k in m] for r in range(N)])
    return p // 2, c * rng.choice([-1.0, 1.0], 8)
def planted(case, rng):
    a, b = np.zeros(C, int), np.full(C, 100)
    if case < 3:
        a = rng.permutation(C)
        b = np.roll(a, [V, -V, int(rng.integers(-V, V + 1))][case])
    elif 3 < case < 7:
        n = C // (2 * V + 2)
        j = [np.array([0]), np.array([C - 1]), np.arange(n) * (2 * V + 2) + rng.integers(2 * V + 2)][case - 4]
        e = [np.array([-V]), np.array([V]), rng.permutation(np.concatenate([[-V, V], rng.integers(1 - V, V, n - 2)]))][case - 4]
        a[j] = 40
        b[(j + e) % C] = 50
    elif case == 7:
        a, b = rng.integers(0, 40, C), rng.integers(0, 40, C)
    return a, b
def setup_inputs(rng):
    return {**numbers_of(rng), **weights(rng)}
def setup_inputs_ties(rng):
    d = numbers_of(rng)
    x = d["x"].reshape(N, 8, 16, C, 4)
    u = d["u"].reshape(N, 8, 16, 128, 4)
    a = x[0][:, :8, :3].copy()
    a[:, :, 2] = 0
    e = int(rng.integers(N))
    for r in range(N):
        k = np.full(C, rng.integers(2)) if r in (e, e ^ STEP[R - 1]) else rng.permutation(C) % 3
        x[r][:, :8] = a[:, :, k]
    x[e ^ STEP[1]] = 0
    u[1:] = u[0]
    u[:, :, 8:, ::16] = 0
    return {"x": x.reshape(N, 128, 4 * C), "u": u.reshape(N, 128, 512), "v": d["v"], **weights(rng, range(8))}
def setup_inputs_near(rng):
    d = numbers_of(rng)
    o, c = signs(rng)
    x = d["x"].astype(np.float32).reshape(N, 8, 16, C, 4)
    u = d["u"].reshape(N, 128, 128, 4)
    size = np.where(o < 2, 2.0 ** -23, 2.0 ** -27)
    x[:, :, 0] = 0
    x[:, :, 8:] = 0
    x[:, :, 0, :, 0] = (c * (o < 2))[:, :, None]
    x[:, :, 8:10] = digits(rng.integers(0, 256, (N, 8, C)), 2) * size[:, None, None, None]
    x[:, :, 10, :, 0] = rng.integers(8, 16, (N, 8, C)) * (o == 3)[:, None] * 2.0 ** -30
    u[:, :, ::16] = 0
    for g in range(8):
        h, k = 16 * g, 1.0 if o[g] == 0 else 2.0 ** -30
        u[:, h, h, 0] = k
        u[:, h + 8:h + 10, h] = k
        u[:, h + 10, h, 0] = k
    return {"x": x.reshape(N, 128, 4 * C).astype(BF), "u": u.reshape(N, 128, 512), "v": d["v"], **weights(rng, [0, 8, 9, 10, 11, 12, 13, 14, 15])}
def setup_inputs_huge(rng):
    d = numbers_of(rng)
    o, c = signs(rng)
    n = np.stack([rng.permutation(513)[:C] for r in range(N)])
    i = np.argsort(rng.random((N, 512, C)), axis=1)
    x = (-2.0 ** 30 * np.where(i < n[:, None], 1.0, 0.875)).reshape(N, 128, 4, C).transpose(0, 1, 3, 2)
    u = d["u"].reshape(N, 128, 128, 4)
    u[:, :, ::16] = (2.0 ** 30 * c).astype(np.float32).astype(BF)[:, None, :, None]
    return {"x": np.ascontiguousarray(x).astype(np.float32).reshape(N, 128, 4 * C).astype(BF), "u": u.reshape(N, 128, 512), "v": d["v"], **weights(rng, range(16))}
def setup_inputs_lists(rng):
    d = numbers_of(rng)
    s = np.zeros((N, 8, C), int)
    for r in range(N):
        p = r ^ STEP[R - 1]
        if r < p:
            n = rng.permutation(8)
            for g in range(8): s[r, g], s[p, g] = planted(int(n[g]), rng)
    x = d["x"].astype(np.float32).reshape(N, 8, 16, C, 4)
    u = d["u"].reshape(N, 128, 128, 4)
    x[:, :, 8:] = 0
    x[:, :, 8:11] = digits(s, 3)
    u[:, :, ::16] = 0
    for h in range(0, 128, 16): u[:, h + 8:h + 11, h] = 1
    return {"x": x.reshape(N, 128, 4 * C).astype(BF), "u": u.reshape(N, 128, 512), "v": d["v"], **weights(rng, range(8, 16))}
def setup_inputs_spread(rng):
    d = setup_inputs(rng)
    d["x"] = big(wide(rng, N, 128, 4 * C, cols=6))
    return d
def check_inputs(d):
    b = []
    for k in ("x", "u", "v"):
        a = np.abs(d[k].astype(np.float32))
        if not (np.isfinite(a).all() and ((a == 0) | (a >= 2.0 ** -30) & (a <= 2.0 ** 30)).all()): b.append("a value of " + k)
    if ((d["wc"] & 0x7F) == 0x7F).any(): b.append("a code of wc that is no number")
    none, least, most = [emit(mx_ref.quantize(np.full((128, 16), k, np.float32).astype(BF)))[1][0, 0] for k in (0.0, 2.0 ** -30, 2.0 ** 30)]
    for r in range(N):
        s = mx_ref.live(d["ws"][r])
        if ((s != none) & ((s < least) | (s > most))).any(): b.append("a scale of ws")
        if ((s == none)[:, None, :, None] & ((d["wc"][r].reshape(16, 8, -1, 4) & 0x7F) != 0)).any(): b.append("a code of wc under the scale of zeros")
    return b
def reference(x, u, v, wc, ws):
    qu = [mx_ref.quantize(u[r]) for r in range(N)]
    lay = [pk(wc[r], ws[r]) for r in range(N)]
    now = [x[r] for r in range(N)]
    place = np.arange(C)
    y, od = np.zeros((N, 128, C), np.float32), np.zeros((N, 8, 2 * C), np.float32)
    oc, osc = np.zeros((N, 128, 4 * C), np.uint8), np.zeros((N, 16, C), np.uint8)
    for t in range(R):
        q = [mx_ref.quantize(now[r]) for r in range(N)]
        s = [mx_ref.matmul(qu[r], q[r])[::16] for r in range(N)]
        held = [decode(q[r]) for r in range(N)]
        d = [match(s[r], s[r ^ STEP[t]]) for r in range(N)]
        made = []
        for r in range(N):
            e = r ^ STEP[t]
            l, h = inherit(d[r], d[e])
            p = held[e].astype(BF)
            z = ((gcols(p, (place + l) % C).astype(np.float32) + gcols(p, (place + h) % C).astype(np.float32)) * np.float32(0.5)).astype(BF)
            qz = mx_ref.quantize(z)
            made.append(tile([np.maximum(mx_ref.matmul(pick(lay[r], np.arange(128 * b, 128 * b + 128)), qz), np.float32(0.0)) * np.float32(0.03125) + held[r][:, b::4] for b in range(4)]))
            od[r] = np.concatenate([l, h], axis=1)
        now = made
    for r in range(N):
        last = mx_ref.quantize(now[r])
        y[r] = mx_ref.matmul(mx_ref.quantize(v[r]), last)
        oc[r], osc[r] = emit(last)
    return {"y": y, "od": od, "oc": oc, "osc": osc}

@@ -1,0 +1,431 @@
+from concourse.mybir import dt, AluOpType, ActivationFunctionType
+
+C, V, R = 352, 17, 3
+STEP = [1, 2, 4]
+H = C // 2
+CH = C // 16
+ND = 2 * V + 1
+WIN = CH + 2 * V
+CHUNKS = [[3, 5, 7, 7], [8, 7, 7]]
+CMAX = 8
+BIG = 1.0e29
+PW = 400
+F32, BF, I32, U16, QC, QS = "float32", "bfloat16", "int32", "uint16", "float8_e4m3fn_x4", "uint8"
+
+SCRATCH = {"psf": ("psum", [128, 2048], F32), "psw": ("psum", [128, 2048], F32)}
+for _d, _bufs in (
+    (BF, dict(xin=[4 * C], ut=[512], vt=[512], ones=[128], ident=[128], ebig=[2048], nf=[2 * CH * ND],
+              ko=[(CH + 32) * ND], rst=[CMAX * ND], kt=[CMAX * ND], tab=[48], t1=[32], zz=[768], dr3=[18, 32],
+              dnat=[18 * CH], cmpn=[C], dj=[C], okn=[C], nok=[C], okd=[C], h0=[C], lrow=[C + 32], hrow=[C + 32],
+              ttl=[2 * C + 32], tth=[2 * C + 32], p3=[4, PW], tl=[4 * C], yt=[4 * C], xt=[4 * C])),
+    (F32, dict(spad=[16, 32], tsc=[512], gsc=[96], w3=[3, 32], dif=[2 * CH * ND], mn=[2 * CH * ND + 1], o1f=[CH],
+               fl=[32], fh=[32], tr=[4 * C], ysb=[C], pf=[4], j16=[CH], jf=[CH], cnt=[32], ca=[32], cb=[32],
+               c1=[CH], plc=[32])),
+    (I32, dict(ig=[6], ig2=[6], pi=[4], ia=[32], ib=[32], ic=[32])),
+    (U16, dict(off1=[CH], off2=[CH], offl=[32], offh=[32], offg=[6], offz=[4], offp=[CH], offt=[2])),
+    (QC, dict(qu=[128], qv=[128], qw=[512], qe=[512], qy=[C])),
+    (QS, dict(su=[128], sv=[128], sw=[512], se=[512], sy=[C])),
+):
+    for _n, _s in _bufs.items():
+        SCRATCH[_n] = ("sbuf", [128] + _s, _d)
+for _t in range(R + 1):
+    SCRATCH["qx%d" % _t] = ("sbuf", [128, C], QC)
+    SCRATCH["sx%d" % _t] = ("sbuf", [128, C], QS)
+for _t in range(R):
+    SCRATCH["ql%d" % _t] = ("sbuf", [128, C], QC)
+    SCRATCH["sl%d" % _t] = ("sbuf", [128, C], QS)
+    SCRATCH["rq%d" % _t] = ("sbuf", [128, H], QC)
+    SCRATCH["rs%d" % _t] = ("sbuf", [128, H], QS)
+    SCRATCH["wo%d" % _t] = ("sbuf", [128, 3 * CH], F32)
+    SCRATCH["wp%d" % _t] = ("sbuf", [128, WIN], F32)
+
+SEMAPHORES = ["pe", "dve", "act", "pool", "sent", "sent0"] + ["dma%d" % i for i in range(24)]
+for _t in range(R):
+    SEMAPHORES += ["asc%d" % _t, "adir%d" % _t, "ahop%d" % _t, "rc%d" % _t, "rsc%d" % _t]
+
+A = AluOpType
+ACT = ActivationFunctionType
+
+
+def helper_of(core, T, topo):
+    r = T.rank_of(core)
+    for c in topo.cores_of(core):
+        if topo.die(c) != topo.die(core) and T.rank_of(c) is None and all(
+                topo.may_write(c, T.cores[r ^ s]) for s in STEP):
+            return c
+    raise ValueError("no helper core")
+
+
+def bits(engines):
+    return sum(1 << e for e in engines)
+
+
+def u8(view):
+    return view.bitcast(dt.uint8)
+
+
+def helper_program(g, core, rank, T, topo):
+    total = 0
+    for t in range(R):
+        dst = T.cores[rank ^ STEP[t]]
+        rid, pid = topo.addr(dst, core)
+        m = topo.mask(core, dst)
+        n = len(topo.engines(core, dst))
+        g.wait_ge(T.sem["rsc%d" % t], n)
+        g.remote_dma(T["sl%d" % t][:, 0:H], T["rs%d" % t][:], T.sem["ahop%d" % t], T.sem.sent, pid, rid, m)
+        g.wait_ge(T.sem["rc%d" % t], n)
+        g.remote_dma(u8(T["ql%d" % t][:, 0:H]), u8(T["rq%d" % t][:]), T.sem["ahop%d" % t], T.sem.sent, pid, rid, m)
+        total += 2 * n
+    g.wait_ge(T.sem.sent, total)
+
+
+def rank_program(g, core, T, topo):
+    rank = T.rank_of(core)
+    if rank is None:
+        for r, c in enumerate(T.cores):
+            if helper_of(c, T, topo) == core:
+                helper_program(g, core, r, T, topo)
+        return
+
+    Q = {"pe": g.tensor, "dve": g.vector, "act": g.scalar, "pool": g, "sp": g.sync}
+    known = {e: {} for e in Q}
+    count = {}
+    writer, readers = {}, {}
+    ndma = [0]
+
+    def await_(e, ev):
+        sem, n, snap, _ = ev
+        if known[e].get(sem, 0) >= n:
+            return
+        Q[e].wait_ge(T.sem[sem], n)
+        known[e][sem] = n
+        for s, k in snap.items():
+            if known[e].get(s, 0) < k:
+                known[e][s] = k
+
+    def deps(e, rd, wr):
+        evs = []
+        for k in rd:
+            if k in writer:
+                evs.append(writer[k])
+            if k.startswith("ps"):
+                evs += [x for x in readers.get(k, []) if x[3] != e]
+        for k in wr:
+            if k in writer:
+                evs.append(writer[k])
+            evs += readers.get(k, [])
+        for ev in sorted(evs, key=lambda x: -x[1]):
+            await_(e, ev)
+
+    def note(ev, rd, wr):
+        for k in rd:
+            readers.setdefault(k, []).append(ev)
+        for k in wr:
+            writer[k] = ev
+            readers[k] = []
+
+    def op(e, fn, rd, wr):
+        deps(e, rd, wr)
+        count[e] = count.get(e, 0) + 1
+        fn().then_inc(T.sem[e], 1)
+        note((e, count[e], dict(known[e]), e), rd, wr)
+
+    def dma(e, out, in_, rd, wr):
+        deps(e, rd, wr)
+        sem = "dma%d" % ndma[0]
+        ndma[0] += 1
+        count[sem] = 16
+        Q[e].dma_start(out, in_).then_inc(T.sem[sem], 16)
+        note((sem, 16, dict(known[e]), "dma"), rd, wr)
+
+    def send(out, in_, dst, mask, rsem, rd, lsem="sent"):
+        deps("pool", rd, [])
+        rid, pid = topo.addr(dst, core)
+        g.remote_dma(out, in_, T.sem[rsem], T.sem[lsem], pid, rid, mask)
+        count[lsem] = count.get(lsem, 0) + bin(mask).count("1")
+
+    def arrives(sem, n, keys):
+        count[sem] = n
+        for k in keys:
+            writer[k] = (sem, n, {}, "far")
+
+    v, s, pe = g.vector, g.scalar, g.tensor
+
+    def vec(fn, rd, wr):
+        op("dve", fn, rd, wr)
+
+    def act(out, in_, f, rd, wr, **kw):
+        op("act", lambda: s.activation(out, in_, f, **kw), rd, wr)
+
+    def ts(out, in0, s1, s2, op0, op1, rd, wr):
+        if op1 is None:
+            vec(lambda: v.tensor_scalar(out, in0, s1, None, op0), rd, wr)
+        else:
+            vec(lambda: v.tensor_scalar(out, in0, s1, s2, op0, op1), rd, wr)
+
+    def tt(out, in0, in1, o, rd, wr):
+        vec(lambda: v.tensor_tensor(out, in0, in1, o), rd, wr)
+
+    def cp(out, in_, rd, wr):
+        vec(lambda: v.tensor_copy(out, in_), rd, wr)
+
+    def turn(out, in_, rd, wr):
+        vec(lambda: v.transpose(out, in_), rd, wr)
+
+    def scan(out, d0, d1, init, op0, op1, rd, wr):
+        vec(lambda: v.tensor_tensor_scan(out, d0, d1, init, op0, op1), rd, wr)
+
+    def fill(ap, val, wr):
+        vec(lambda: v.memset(ap, val), [], wr)
+
+    def mm(ps, bank, lq, ls, l0, rq, rs, r0, n, rd):
+        op("pe", lambda: pe.matmul_mx(T[ps][:, 512 * bank:512 * bank + n], T[lq][:, l0:l0 + 128], T[ls][:, l0:l0 + 128],
+                                      T[rq][:, r0:r0 + n], T[rs][:, r0:r0 + n], True, True), rd, ["%s%d" % (ps, bank)])
+
+    def quant(q, sc, src, c0, n, rd, wr):
+        vec(lambda: v.quantize_mx(T[q][:, c0:c0 + n], T[sc][:, c0:c0 + n], T[src][:, 4 * c0:4 * (c0 + n)]), rd, wr)
+
+    def iota(out, pat, base, cm, wr, small=False):
+        if small:
+            op("pool", lambda: g.iota(out, pat, base, cm, allow_small_or_imprecise_dtypes=True), [], wr)
+        else:
+            op("pool", lambda: g.iota(out, pat, base, cm), [], wr)
+
+    helper = helper_of(core, T, topo)
+    near = topo.engines(core, helper)
+    far = topo.engines(core, T.cores[rank ^ STEP[0]])
+    inner = [e for e in near if e not in far]
+    nfar = len(far)
+
+    dma("sp", T.xin[:, 0:4 * H], T.x[:, 0:4 * H], [], ["xin0"])
+    dma("act", T.ut[:], T.u[:], [], ["ut"])
+    dma("sp", T.xin[:, 4 * H:4 * C], T.x[:, 4 * H:4 * C], [], ["xin1"])
+    fill(T.ones[:], 1.0, ["ones"])
+    fill(T.spad[:], 0.0, ["spad0", "spad1"])
+    iota(T.ig[:], [[32, 3], [16, 2]], 32 * 15, 32, ["ig"])
+    iota(T.kt[:], [[0, CMAX], [-1, ND]], ND, 0, ["kt"], True)
+    iota(T.pi[:, 0:1], [[0, 1]], 0, 1, ["pi0"])
+    iota(T.j16[:], [[16, CH]], 0, 0, ["j16"], True)
+    iota(T.cnt[:], [[1, 32]], 0, 0, ["cnt"], True)
+    iota(T.tab[:], [[-1, 48]], ND + 1, 0, ["tab"], True)
+    op("pool", lambda: g.affine_select(T.ident[:], T.ones[:], [[-1, 128]], A.is_equal, 0.0, 0, 1), ["ones"], ["ident"])
+    fill(T.mn[:, 0:1], 0.0, ["mnp"])
+    fill(T.ko[:, 2 * CH * ND:(CH + 32) * ND], 0.0, ["kop"])
+    fill(T.zz[:], 0.0, ["zz"])
+    ts(T.ig2[:], T.ig[:], 511, None, A.bitwise_and, None, ["ig"], ["ig2"])
+    fill(T.lrow[:], 0.0, ["lrow"])
+    fill(T.hrow[:], 0.0, ["hrow"])
+    cp(T.offg[:], T.ig2[:], ["ig2"], ["offg"])
+    ts(T.rst[:], T.kt[:], float(ND), BIG, A.is_equal, A.mult, ["kt"], ["rst"])
+    quant("qu", "su", "ut", 0, 128, ["ut"], ["qu"])
+
+    def late_constants():
+        ts(T.pi[:, 1:2], T.pi[:, 0:1], 15, None, A.bitwise_and, None, ["pi0"], ["pi1"])
+        ts(T.pi[:, 2:3], T.pi[:, 0:1], 4, 1, A.arith_shift_right, A.bitwise_and, ["pi0"], ["pi2"])
+        fill(T.ebig[:], 0.0, ["ebig"])
+        cp(T.pf[:, 0:1], T.pi[:, 1:2], ["pi1"], ["pf0"])
+        cp(T.pf[:, 2:3], T.pi[:, 2:3], ["pi2"], ["pf2"])
+        ts(T.pf[:, 1:2], T.pi[:, 1:2], float(CH), None, A.mult, None, ["pi1"], ["pf1"])
+        ts(T.pf[:, 3:4], T.pi[:, 2:3], 16.0, None, A.mult, None, ["pi2"], ["pf3"])
+        ts(T.jf[:], T.j16[:], T.pf[:, 0:1], None, A.add, None, ["j16", "pf0"], ["jf"])
+        ts(T.c1[:], T.cnt[:, 0:CH], T.pf[:, 1:2], float(CH + V + 1), A.add, A.add, ["cnt", "pf1"], ["c1"])
+        for b in range(4):
+            cp(T.ebig[:, 512 * b + b:512 * (b + 1):4], T.ident[:], ["ident", "ebig"], ["e%d" % b])
+        ts(T.ia[:, 0:4], T.jf[:, 0:4], 30.0, None, A.add, None, ["jf"], ["ia"])
+        ts(T.ca[:, 0:CH], T.jf[:], -0.5 * (CH - 1), 1.0 / CH, A.add, A.mult, ["jf"], ["ca"])
+        ts(T.ib[:, 0:4], T.ia[:, 0:4], 1, 15, A.arith_shift_right, A.bitwise_and, ["ia"], ["ib"])
+        ts(T.ic[:, 0:4], T.ia[:, 0:4], 1, None, A.bitwise_and, None, ["ia"], ["ic"])
+        cp(T.ia[:, 0:CH], T.ca[:, 0:CH], ["ca"], ["ia"])
+        ts(T.ic[:, 4:8], T.ic[:, 0:4], 16.0, None, A.mult, None, ["ic"], ["ic4"])
+        ts(T.cb[:, 0:CH], T.jf[:], 16.0, None, A.mult, None, ["jf"], ["cb"])
+        ts(T.ca[:, 0:CH], T.ia[:, 0:CH], float(1 - C), None, A.mult, None, ["ia"], ["ca"])
+        tt(T.ib[:, 4:8], T.ib[:, 0:4], T.ic[:, 4:8], A.add, ["ib", "ic4"], ["ib4"])
+        tt(T.ca[:, 0:CH], T.ca[:, 0:CH], T.cb[:, 0:CH], A.add, ["ca", "cb"], ["ca"])
+        cp(T.offz[:], T.ib[:, 4:8], ["ib4"], ["offz"])
+        cp(T.offp[:], T.ca[:, 0:CH], ["ca"], ["offp"])
+        ts(T.cb[:], T.cnt[:], 12.0, -1.0, A.is_ge, A.mult, ["cnt"], ["cb"])
+        ts(T.ca[:, 0:2], T.jf[:, 0:2], 12.0, -1.0, A.is_ge, A.mult, ["jf"], ["ca"])
+        for b in range(2):
+            quant("qe", "se", "ebig", 128 * b, 128, ["e%d" % b], ["qe%d" % b])
+        tt(T.cb[:], T.cb[:], T.cnt[:], A.add, ["cb", "cnt"], ["cb"])
+        tt(T.ca[:, 0:2], T.ca[:, 0:2], T.jf[:, 0:2], A.add, ["ca", "jf"], ["ca"])
+        ts(T.cb[:], T.cb[:], 16.0, float(V), A.mult, A.add, ["cb"], ["cb"])
+        ts(T.ca[:, 0:2], T.ca[:, 0:2], float(CH), 1.0, A.min, A.add, ["ca"], ["ca"])
+        ts(T.plc[:], T.cb[:], T.pf[:, 0:1], None, A.add, None, ["cb", "pf0"], ["plc"])
+        ts(T.ia[:, 0:2], T.ca[:, 0:2], T.pf[:, 2:3], None, A.subtract, None, ["ca", "pf2"], ["ia"])
+        for b in range(2, 4):
+            quant("qe", "se", "ebig", 128 * b, 128, ["e%d" % b], ["qe%d" % b])
+        ts(T.ib[:, 0:2], T.ia[:, 0:2], 1, None, A.arith_shift_right, None, ["ia"], ["ib"])
+        ts(T.ic[:, 0:2], T.ia[:, 0:2], 1, None, A.bitwise_and, None, ["ia"], ["ic"])
+        ts(T.ca[:, 0:2], T.ib[:, 0:2], 32.0, T.pf[:, 3:4], A.mult, A.add, ["ib", "pf3"], ["ca"])
+        ts(T.cb[:, 0:2], T.ic[:, 0:2], float(-C), float(C), A.mult, A.add, ["ic"], ["cb"])
+        tt(T.ca[:, 0:2], T.ca[:, 0:2], T.cb[:, 0:2], A.add, ["ca", "cb"], ["ca"])
+        cp(T.offt[:], T.ca[:, 0:2], ["ca"], ["offt"])
+
+    def first_half_out(t):
+        send(u8(T["rq%d" % t][:]), u8(T["qx%d" % t][:, 0:H]), helper, bits(inner), "rc%d" % t, ["qx%d0" % t])
+        send(T["rs%d" % t][:], T["sx%d" % t][:, 0:H], helper, bits(far), "rsc%d" % t, ["qx%d0" % t])
+
+    def side_product(t, h, q, sc):
+        mm("psw", h, q, sc, 0, "qx%d" % t, "sx%d" % t, h * H, H, [q, "qx%d%d" % (t, h)])
+
+    for h in range(2):
+        quant("qx0", "sx0", "xin", h * H, H, ["xin%d" % h], ["qx0%d" % h])
+        side_product(0, h, "qu", "su")
+        if h == 0:
+            first_half_out(0)
+
+    for t in range(R):
+        partner = T.cores[rank ^ STEP[t]]
+        qx, sx, ql, sl = "qx%d" % t, "sx%d" % t, "ql%d" % t, "sl%d" % t
+        kwo, kwp = "wo%d" % t, "wp%d" % t
+        wo, wp = T[kwo], T[kwp]
+        for h in range(2):
+            act(T.spad[:, 8 * h:8 * h + 8, 0:CH], T.psw[:, 512 * h:512 * h + H], ACT.Copy,
+                ["psw%d" % h], ["spad%d" % h])
+            turn(T.tsc[:, 256 * h:256 * h + 256], T.spad[:, 8 * h:8 * h + 8, :], ["spad%d" % h], ["tsc%d" % h])
+        cp(T.gsc[:], T.tsc[:].indirect(T.offg[:]), ["tsc0", "tsc1", "offg"], ["gsc"])
+        turn(T.w3[:], T.gsc[:], ["gsc"], ["w3"])
+        cp(wo[:], T.w3[:, :, 0:CH], ["w3"], [kwo])
+        w0 = CH - V
+        m = topo.mask(core, partner)
+        send(wp[:], wo[:, w0:w0 + WIN], partner, m, "asc%d" % t, [kwo], "sent0" if t == 0 else "sent")
+        send(u8(T[ql][:, H:C]), u8(T[qx][:, H:C]), partner, m, "adir%d" % t, [qx + "1"])
+        send(T[sl][:, H:C], T[sx][:, H:C], partner, m, "adir%d" % t, [qx + "1"])
+        arrives("asc%d" % t, nfar, [kwp])
+        arrives("adir%d" % t, 2 * nfar, [ql + "1"])
+        arrives("ahop%d" % t, 2 * nfar, [ql + "0"])
+        if t == 0:
+            await_("sp", ("sent0", count["sent0"], {}, "far"))
+            dma("sp", u8(T.qw[:]), T.wc[:], [], ["qw"])
+            dma("sp", T.sw[:], T.ws[:], [], ["sw"])
+            dma("sp", T.vt[:], T.v[:], [], ["vt"])
+            late_constants()
+        if t == 1:
+            quant("qv", "sv", "vt", 0, 128, ["vt"], ["qv"])
+        for b in range(4):
+            mm("psf", b, "qe", "se", 128 * b, qx, sx, 0, C, ["qe%d" % b, qx + "0", qx + "1"])
+        for b in range(4):
+            mm("psw", b, "qe", "se", 128 * b, ql, sl, 0, C, ["qe%d" % b, ql + "0", ql + "1"])
+
+        steps = []
+        for d in range(2):
+            i0 = 0
+            for n in CHUNKS[d]:
+                steps.append((d, i0, n))
+                i0 += n
+
+        def span(c):
+            d, i0, n = steps[c]
+            return (d * CH + i0) * ND, (d * CH + i0 + n) * ND
+
+        def least(c):
+            d, i0, n = steps[c]
+            a, e = span(c)
+            scan(T.mn[:, 1 + a:1 + e], T.rst[:, 0:e - a], T.dif[:, a:e], 0.0, A.add, A.min,
+                 ["rst"] + ["dif%d_%d" % (d, i) for i in range(i0, i0 + n)], ["mn%d" % c])
+
+        for d in range(2):
+            for i in range(CH):
+                a = (d * CH + i) * ND
+                if d == 0:
+                    win, mid = wp[:, i:i + ND], wo[:, CH + i:CH + i + 1]
+                else:
+                    win, mid = wo[:, w0 + i:w0 + i + ND], wp[:, V + i:V + i + 1]
+                act(T.dif[:, a:a + ND], win, ACT.Abs, [kwo, kwp], ["dif%d_%d" % (d, i)], bias=mid, scale=-1.0)
+
+        n0, nall = len(CHUNKS[0]), len(steps)
+        k0 = ["ko%d" % c for c in range(n0)]
+        k1 = ["ko%d" % c for c in range(n0, nall)]
+        own = T.ko[:, ND - 1:CH * ND:ND]
+        least(0)
+        for c in range(nall):
+            a, e = span(c)
+            tt(T.nf[:, a:e], T.mn[:, 1 + a:1 + e], T.mn[:, a:e], A.is_equal,
+               ["mn%d" % c, "mn%d" % (c - 1) if c else "mnp"], ["nf%d" % c])
+            if c + 1 < nall:
+                least(c + 1)
+            if c == n0:
+                cp(T.off2[:], own, k0, ["off2"])
+                tt(T.o1f[:], T.c1[:], own, A.subtract, ["c1"] + k0, ["o1f"])
+            scan(T.ko[:, a:e], T.nf[:, a:e], T.kt[:, 0:e - a], 0.0, A.mult, A.max, ["nf%d" % c, "kt"], ["ko%d" % c])
+            if c == n0:
+                cp(T.off1[:], T.o1f[:], ["o1f"], ["off1"])
+        act(T.cmpn[:], T.tab[:].indirect(T.off2[:]), ACT.Copy, ["tab", "off2"], ["cmpn"])
+        act(T.dj[:], T.cmpn[:].indirect(T.offp[:]), ACT.Identity, ["cmpn", "offp"], ["dj"], bias=-float(V + 1))
+
+        def unpack(b):
+            act(T.p3[:, b, V:V + C], T.psw[:, 512 * b:512 * b + C], ACT.Copy, ["psw%d" % b], ["p3_%d" % b], scale=0.5)
+
+        unpack(0)
+        unpack(1)
+        turn(T.t1[:], T.ko[:, CH * ND + ND - 1:(CH + 32) * ND:ND], k1 + ["kop"], ["t1"])
+        cp(T.zz[:, 0:768:16], T.t1[:].indirect(T.offz[:, 0:3]), ["t1", "offz"], ["zz"])
+        turn(T.dr3[:], T.zz[:, 0:576], ["zz"], ["dr3"])
+        cp(T.dnat[:], T.dr3[:, :, 0:CH], ["dr3"], ["dnat"])
+        tt(T.okn[:], T.dnat[:].indirect(T.off1[:]), T.cmpn[:], A.is_equal, ["dnat", "off1", "cmpn"], ["okn"])
+        act(T.nok[:], T.okn[:].indirect(T.offp[:]), ACT.Identity, ["okn", "offp"], ["nok"], bias=1.0, scale=-1.0)
+        tt(T.okd[:], T.okn[:].indirect(T.offp[:]), T.dj[:], A.mult, ["okn", "offp", "dj"], ["okd"])
+        unpack(2)
+        unpack(3)
+        planes = ["p3_%d" % b for b in range(4)]
+        act(T.p3[:, :, 0:V], T.p3[:, :, C:C + V], ACT.Copy, planes, ["p3a"])
+        act(T.p3[:, :, V + C:PW], T.p3[:, :, V:PW - C], ACT.Copy, planes, ["p3b"])
+        planes += ["p3a", "p3b"]
+
+        scan(T.h0[:, ::-1], T.nok[:, ::-1], T.okd[:, ::-1], 0.0, A.mult, A.add, ["nok", "okd"], ["h0"])
+        scan(T.lrow[:, 16:16 + C], T.nok[:], T.okd[:], T.h0[:, 0:1], A.mult, A.add, ["nok", "okd", "h0"], ["lrow"])
+
+        def to_list(row, tb, f, off):
+            turn(T[tb][:, 0:C], T[row][:, 16:16 + C], [row], [tb + "a"])
+            turn(T[tb][:, C:2 * C + 32], T[row][:], [row], [tb + "b"])
+            tt(T[f][:], T[tb][:].indirect(T.offt[:]), T.plc[:], A.add, [tb + "a", tb + "b", "offt", "plc"], [f])
+            cp(T[off][:], T[f][:], [f], [off])
+
+        to_list("lrow", "ttl", "fl", "offl")
+        scan(T.hrow[:, 15 + C:15:-1], T.nok[:, ::-1], T.okd[:, ::-1], T.lrow[:, 15 + C:16 + C], A.mult, A.add,
+             ["nok", "okd", "lrow"], ["hrow"])
+        to_list("hrow", "tth", "fh", "offh")
+        if t == R - 1:
+            dma("pool", T.od[:, 0:C], T.lrow[0:128:16, 16:16 + C], ["lrow"], [])
+            dma("pool", T.od[:, C:2 * C], T.hrow[0:128:16, 16:16 + C], ["hrow"], [])
+
+        for h in range(2):
+            for b in range(4):
+                a = b * C + h * H
+                act(T.tl[:, a:a + H], T.p3[:, b, :].indirect(T.offl[:, 12 * h:12 * h + 11]), ACT.Copy,
+                    planes + ["offl"], ["tl%d%d" % (h, b)])
+                tt(T.yt[:, 4 * h * H + b:4 * (h + 1) * H:4], T.p3[:, b, :].indirect(T.offh[:, 12 * h:12 * h + 11]),
+                   T.tl[:, a:a + H], A.add, planes + ["offh", "tl%d%d" % (h, b)], ["yt%d%d" % (h, b)])
+            quant("qy", "sy", "yt", h * H, H, ["yt%d%d" % (h, b) for b in range(4)], ["qy%d" % h])
+        for h in range(2):
+            for b in range(4):
+                a = b * C + h * H
+                mm("psw", b, "qw", "sw", 128 * b, "qy", "sy", h * H, H, ["qw", "sw", "qy%d" % h])
+                act(T.tr[:, a:a + H], T.psw[:, 512 * b:512 * b + H], ACT.Relu, ["psw%d" % b], ["tr%d%d" % (h, b)],
+                    scale=0.03125)
+        u = t + 1
+        qn, sn = "qx%d" % u, "sx%d" % u
+        for h in range(2):
+            for b in range(4):
+                a = b * C + h * H
+                tt(T.xt[:, 4 * h * H + b:4 * (h + 1) * H:4], T.tr[:, a:a + H],
+                   T.psf[:, 512 * b + h * H:512 * b + (h + 1) * H], A.add,
+                   ["tr%d%d" % (h, b), "psf%d" % b], ["xt%d%d" % (h, b)])
+            quant(qn, sn, "xt", h * H, H, ["xt%d%d" % (h, b) for b in range(4)], [qn + str(h)])
+            if u < R:
+                side_product(u, h, "qu", "su")
+                if h == 0:
+                    first_half_out(u)
+            else:
+                side_product(u, h, "qv", "sv")
+                dma("sp", T.oc[:, 4 * h * H:4 * (h + 1) * H], u8(T[qn][:, h * H:(h + 1) * H]), [qn + str(h)], [])
+
+    last = ["qx%d0" % R, "qx%d1" % R]
+    for k in range(4):
+        dma("pool" if k % 2 else "sp", T.osc[4 * k:4 * k + 4, :], T["sx%d" % R][32 * k:32 * k + 4, :], last, [])
+    for h in range(2):
+        act(T.ysb[:, h * H:(h + 1) * H], T.psw[:, 512 * h:512 * h + H], ACT.Copy, ["psw%d" % h], ["ysb%d" % h])
+        dma("act", T.y[:, h * H:(h + 1) * H], T.ysb[:, h * H:(h + 1) * H], ["ysb%d" % h], [])
+    for sem, n in count.items():
+        await_("pool", (sem, n, {}, "end"))

@@ -6,23 +6,25 @@ H = C // 2
 CH = C // 16
 ND = 2 * V + 1
 WIN = CH + 2 * V
-CHUNKS = [[3, 5, 7, 7], [8, 7, 7]]
+CHUNKS = [[4, 7, 5, 6], [8, 8, 6]]
 CMAX = 8
+X0, NX, NC = 4, 7, 16
 BIG = 1.0e29
 PW = 400
 F32, BF, I32, U16, QC, QS = "float32", "bfloat16", "int32", "uint16", "float8_e4m3fn_x4", "uint8"
 
 SCRATCH = {"psf": ("psum", [128, 2048], F32), "psw": ("psum", [128, 2048], F32)}
 for _d, _bufs in (
-    (BF, dict(xin=[4 * C], ut=[512], vt=[512], ones=[128], ident=[128], ebig=[2048], nf=[2 * CH * ND],
+    (BF, dict(xin=[4 * C], ut=[512], vt=[512], ones=[128], ident=[128], ebig=[2048], zer=[512], nf=[2 * CH * ND],
               ko=[(CH + 32) * ND], rst=[CMAX * ND], kt=[CMAX * ND], tab=[48], t1=[32], zz=[768], dr3=[18, 32],
               dnat=[18 * CH], cmpn=[C], dj=[C], okn=[C], nok=[C], okd=[C], h0=[C], lrow=[C + 32], hrow=[C + 32],
               ttl=[2 * C + 32], tth=[2 * C + 32], p3=[4, PW], tl=[4 * C], yt=[4 * C], xt=[4 * C])),
     (F32, dict(spad=[16, 32], tsc=[512], gsc=[96], w3=[3, 32], dif=[2 * CH * ND], mn=[2 * CH * ND + 1], o1f=[CH],
                fl=[32], fh=[32], tr=[4 * C], ysb=[C], pf=[4], j16=[CH], jf=[CH], cnt=[32], ca=[32], cb=[32],
-               c1=[CH], plc=[32])),
-    (I32, dict(ig=[6], ig2=[6], pi=[4], ia=[32], ib=[32], ic=[32])),
-    (U16, dict(off1=[CH], off2=[CH], offl=[32], offh=[32], offg=[6], offz=[4], offp=[CH], offt=[2])),
+               c1=[CH], plc=[32], rep=[16 * NC], raw=[16 * NC], cc=[NC], cd=[NC])),
+    (I32, dict(ig=[6], ig2=[6], pi=[4], ia=[32], ib=[32], ic=[32], ie=[NC])),
+    (U16, dict(off1=[CH], off2=[CH], offl=[32], offh=[32], offg=[6], offz=[4], offp=[CH], offt=[2], offa=[NC],
+               offb=[NC])),
     (QC, dict(qu=[128], qv=[128], qw=[512], qe=[512], qy=[C])),
     (QS, dict(su=[128], sv=[128], sw=[512], se=[512], sy=[C])),
 ):
@@ -71,10 +73,11 @@ def helper_program(g, core, rank, T, topo):
         rid, pid = topo.addr(dst, core)
         m = topo.mask(core, dst)
         n = len(topo.engines(core, dst))
-        g.wait_ge(T.sem["rsc%d" % t], n)
-        g.remote_dma(T["sl%d" % t][:, 0:H], T["rs%d" % t][:], T.sem["ahop%d" % t], T.sem.sent, pid, rid, m)
-        g.wait_ge(T.sem["rc%d" % t], n)
-        g.remote_dma(u8(T["ql%d" % t][:, 0:H]), u8(T["rq%d" % t][:]), T.sem["ahop%d" % t], T.sem.sent, pid, rid, m)
+        hops = [("rsc", T["sl%d" % t][:, 0:H], T["rs%d" % t][:]),
+                ("rc", u8(T["ql%d" % t][:, 0:H]), u8(T["rq%d" % t][:]))]
+        for sem, out, in_ in (hops if t == 0 else hops[::-1]):
+            g.wait_ge(T.sem["%s%d" % (sem, t)], n)
+            g.remote_dma(out, in_, T.sem["ahop%d" % t], T.sem.sent, pid, rid, m)
         total += 2 * n
     g.wait_ge(T.sem.sent, total)
 
@@ -201,37 +204,45 @@ def rank_program(g, core, T, topo):
     dma("act", T.ut[:], T.u[:], [], ["ut"])
     dma("sp", T.xin[:, 4 * H:4 * C], T.x[:, 4 * H:4 * C], [], ["xin1"])
     fill(T.ones[:], 1.0, ["ones"])
-    fill(T.spad[:], 0.0, ["spad0", "spad1"])
+    fill(T.zer[:], 0.0, ["zer"])
+    fill(T.zz[:], 0.0, ["zz"])
     iota(T.ig[:], [[32, 3], [16, 2]], 32 * 15, 32, ["ig"])
-    iota(T.kt[:], [[0, CMAX], [-1, ND]], ND, 0, ["kt"], True)
     iota(T.pi[:, 0:1], [[0, 1]], 0, 1, ["pi0"])
     iota(T.j16[:], [[16, CH]], 0, 0, ["j16"], True)
     iota(T.cnt[:], [[1, 32]], 0, 0, ["cnt"], True)
+    iota(T.kt[:], [[0, CMAX], [-1, ND]], ND, 0, ["kt"], True)
     iota(T.tab[:], [[-1, 48]], ND + 1, 0, ["tab"], True)
     op("pool", lambda: g.affine_select(T.ident[:], T.ones[:], [[-1, 128]], A.is_equal, 0.0, 0, 1), ["ones"], ["ident"])
+    act(T.spad[:], T.zer[:], ACT.Copy, ["zer"], ["spad0", "spad1"])
+    act(T.lrow[:], T.zer[:, 0:C + 32], ACT.Copy, ["zer"], ["lrow"])
+    act(T.hrow[:], T.zer[:, 0:C + 32], ACT.Copy, ["zer"], ["hrow"])
     fill(T.mn[:, 0:1], 0.0, ["mnp"])
     fill(T.ko[:, 2 * CH * ND:(CH + 32) * ND], 0.0, ["kop"])
-    fill(T.zz[:], 0.0, ["zz"])
     ts(T.ig2[:], T.ig[:], 511, None, A.bitwise_and, None, ["ig"], ["ig2"])
-    fill(T.lrow[:], 0.0, ["lrow"])
-    fill(T.hrow[:], 0.0, ["hrow"])
+    ts(T.pi[:, 1:2], T.pi[:, 0:1], 15, None, A.bitwise_and, None, ["pi0"], ["pi1"])
+    ts(T.pi[:, 2:3], T.pi[:, 0:1], 4, 1, A.arith_shift_right, A.bitwise_and, ["pi0"], ["pi2"])
     cp(T.offg[:], T.ig2[:], ["ig2"], ["offg"])
+    cp(T.pf[:, 0:1], T.pi[:, 1:2], ["pi1"], ["pf0"])
+    cp(T.pf[:, 2:3], T.pi[:, 2:3], ["pi2"], ["pf2"])
+    ts(T.pf[:, 1:2], T.pi[:, 1:2], float(CH), None, A.mult, None, ["pi1"], ["pf1"])
+    ts(T.jf[:], T.j16[:], T.pf[:, 0:1], None, A.add, None, ["j16", "pf0"], ["jf"])
+    ts(T.pf[:, 3:4], T.pi[:, 2:3], 16.0, None, A.mult, None, ["pi2"], ["pf3"])
+    ts(T.cc[:], T.jf[:, 0:NC], -float(V), 1.0 / ND, A.add, A.mult, ["jf"], ["cc"])
+    ts(T.c1[:], T.cnt[:, 0:CH], T.pf[:, 1:2], float(CH + V + 1), A.add, A.add, ["cnt", "pf1"], ["c1"])
+    cp(T.ie[:], T.cc[:], ["cc"], ["ie"])
+    ts(T.ia[:, 0:4], T.jf[:, 0:4], 30.0, None, A.add, None, ["jf"], ["ia"])
+    ts(T.cd[:], T.ie[:], float(1 - ND), float(X0), A.mult, A.add, ["ie"], ["cd"])
+    ts(T.offa[:], T.ie[:], float(CH + X0), None, A.add, None, ["ie"], ["offa"])
+    tt(T.cc[:], T.cd[:], T.jf[:, 0:NC], A.add, ["cd", "jf"], ["cc"])
     ts(T.rst[:], T.kt[:], float(ND), BIG, A.is_equal, A.mult, ["kt"], ["rst"])
+    cp(T.offb[:], T.cc[:], ["cc"], ["offb"])
     quant("qu", "su", "ut", 0, 128, ["ut"], ["qu"])
 
     def late_constants():
-        ts(T.pi[:, 1:2], T.pi[:, 0:1], 15, None, A.bitwise_and, None, ["pi0"], ["pi1"])
-        ts(T.pi[:, 2:3], T.pi[:, 0:1], 4, 1, A.arith_shift_right, A.bitwise_and, ["pi0"], ["pi2"])
-        fill(T.ebig[:], 0.0, ["ebig"])
-        cp(T.pf[:, 0:1], T.pi[:, 1:2], ["pi1"], ["pf0"])
-        cp(T.pf[:, 2:3], T.pi[:, 2:3], ["pi2"], ["pf2"])
-        ts(T.pf[:, 1:2], T.pi[:, 1:2], float(CH), None, A.mult, None, ["pi1"], ["pf1"])
-        ts(T.pf[:, 3:4], T.pi[:, 2:3], 16.0, None, A.mult, None, ["pi2"], ["pf3"])
-        ts(T.jf[:], T.j16[:], T.pf[:, 0:1], None, A.add, None, ["j16", "pf0"], ["jf"])
-        ts(T.c1[:], T.cnt[:, 0:CH], T.pf[:, 1:2], float(CH + V + 1), A.add, A.add, ["cnt", "pf1"], ["c1"])
         for b in range(4):
-            cp(T.ebig[:, 512 * b + b:512 * (b + 1):4], T.ident[:], ["ident", "ebig"], ["e%d" % b])
-        ts(T.ia[:, 0:4], T.jf[:, 0:4], 30.0, None, A.add, None, ["jf"], ["ia"])
+            act(T.ebig[:, 512 * b:512 * (b + 1)], T.zer[:], ACT.Copy, ["zer"], ["e%d" % b])
+        for b in range(4):
+            act(T.ebig[:, 512 * b + b:512 * (b + 1):4], T.ident[:], ACT.Copy, ["ident"], ["e%d" % b])
         ts(T.ca[:, 0:CH], T.jf[:], -0.5 * (CH - 1), 1.0 / CH, A.add, A.mult, ["jf"], ["ca"])
         ts(T.ib[:, 0:4], T.ia[:, 0:4], 1, 15, A.arith_shift_right, A.bitwise_and, ["ia"], ["ib"])
         ts(T.ic[:, 0:4], T.ia[:, 0:4], 1, None, A.bitwise_and, None, ["ia"], ["ic"])
@@ -245,26 +256,24 @@ def rank_program(g, core, T, topo):
         cp(T.offp[:], T.ca[:, 0:CH], ["ca"], ["offp"])
         ts(T.cb[:], T.cnt[:], 12.0, -1.0, A.is_ge, A.mult, ["cnt"], ["cb"])
         ts(T.ca[:, 0:2], T.jf[:, 0:2], 12.0, -1.0, A.is_ge, A.mult, ["jf"], ["ca"])
-        for b in range(2):
-            quant("qe", "se", "ebig", 128 * b, 128, ["e%d" % b], ["qe%d" % b])
         tt(T.cb[:], T.cb[:], T.cnt[:], A.add, ["cb", "cnt"], ["cb"])
         tt(T.ca[:, 0:2], T.ca[:, 0:2], T.jf[:, 0:2], A.add, ["ca", "jf"], ["ca"])
         ts(T.cb[:], T.cb[:], 16.0, float(V), A.mult, A.add, ["cb"], ["cb"])
         ts(T.ca[:, 0:2], T.ca[:, 0:2], float(CH), 1.0, A.min, A.add, ["ca"], ["ca"])
         ts(T.plc[:], T.cb[:], T.pf[:, 0:1], None, A.add, None, ["cb", "pf0"], ["plc"])
         ts(T.ia[:, 0:2], T.ca[:, 0:2], T.pf[:, 2:3], None, A.subtract, None, ["ca", "pf2"], ["ia"])
-        for b in range(2, 4):
-            quant("qe", "se", "ebig", 128 * b, 128, ["e%d" % b], ["qe%d" % b])
         ts(T.ib[:, 0:2], T.ia[:, 0:2], 1, None, A.arith_shift_right, None, ["ia"], ["ib"])
         ts(T.ic[:, 0:2], T.ia[:, 0:2], 1, None, A.bitwise_and, None, ["ia"], ["ic"])
         ts(T.ca[:, 0:2], T.ib[:, 0:2], 32.0, T.pf[:, 3:4], A.mult, A.add, ["ib", "pf3"], ["ca"])
         ts(T.cb[:, 0:2], T.ic[:, 0:2], float(-C), float(C), A.mult, A.add, ["ic"], ["cb"])
         tt(T.ca[:, 0:2], T.ca[:, 0:2], T.cb[:, 0:2], A.add, ["ca", "cb"], ["ca"])
         cp(T.offt[:], T.ca[:, 0:2], ["ca"], ["offt"])
+        for b in range(4):
+            quant("qe", "se", "ebig", 128 * b, 128, ["e%d" % b], ["qe%d" % b])
 
     def first_half_out(t):
         send(u8(T["rq%d" % t][:]), u8(T["qx%d" % t][:, 0:H]), helper, bits(inner), "rc%d" % t, ["qx%d0" % t])
-        send(T["rs%d" % t][:], T["sx%d" % t][:, 0:H], helper, bits(far), "rsc%d" % t, ["qx%d0" % t])
+        send(T["rs%d" % t][:], T["sx%d" % t][:, 0:H], helper, bits(inner if t else far), "rsc%d" % t, ["qx%d0" % t])
 
     def side_product(t, h, q, sc):
         mm("psw", h, q, sc, 0, "qx%d" % t, "sx%d" % t, h * H, H, [q, "qx%d%d" % (t, h)])
@@ -325,9 +334,16 @@ def rank_program(g, core, T, topo):
             scan(T.mn[:, 1 + a:1 + e], T.rst[:, 0:e - a], T.dif[:, a:e], 0.0, A.add, A.min,
                  ["rst"] + ["dif%d_%d" % (d, i) for i in range(i0, i0 + n)], ["mn%d" % c])
 
+        act(T.rep[:], wo[:].indirect(T.offa[:]), ACT.Copy, [kwo, "offa"], ["rep"])
+        tt(T.raw[:], wp[:].indirect(T.offb[:]), T.rep[:], A.subtract, [kwp, "offb", "rep"], ["raw"])
         for d in range(2):
             for i in range(CH):
                 a = (d * CH + i) * ND
+                if d == 0 and X0 <= i < X0 + NX:
+                    if i == X0:
+                        act(T.dif[:, a:a + NX * ND], T.raw[:, 0:NX * ND], ACT.Abs, ["raw"],
+                            ["dif0_%d" % k for k in range(X0, X0 + NX)])
+                    continue
                 if d == 0:
                     win, mid = wp[:, i:i + ND], wo[:, CH + i:CH + i + 1]
                 else:
@@ -361,9 +377,11 @@ def rank_program(g, core, T, topo):
         unpack(1)
         turn(T.t1[:], T.ko[:, CH * ND + ND - 1:(CH + 32) * ND:ND], k1 + ["kop"], ["t1"])
         cp(T.zz[:, 0:768:16], T.t1[:].indirect(T.offz[:, 0:3]), ["t1", "offz"], ["zz"])
-        turn(T.dr3[:], T.zz[:, 0:576], ["zz"], ["dr3"])
-        cp(T.dnat[:], T.dr3[:, :, 0:CH], ["dr3"], ["dnat"])
-        tt(T.okn[:], T.dnat[:].indirect(T.off1[:]), T.cmpn[:], A.is_equal, ["dnat", "off1", "cmpn"], ["okn"])
+        for h in range(2):
+            turn(T.dr3[:, 9 * h:9 * h + 9, :], T.zz[:, 288 * h:288 * h + 288], ["zz"], ["dr3%d" % h])
+        for h in range(2):
+            cp(T.dnat[:, 9 * CH * h:9 * CH * (h + 1)], T.dr3[:, 9 * h:9 * h + 9, 0:CH], ["dr3%d" % h], ["dnat%d" % h])
+        tt(T.okn[:], T.dnat[:].indirect(T.off1[:]), T.cmpn[:], A.is_equal, ["dnat0", "dnat1", "off1", "cmpn"], ["okn"])
         act(T.nok[:], T.okn[:].indirect(T.offp[:]), ACT.Identity, ["okn", "offp"], ["nok"], bias=1.0, scale=-1.0)
         tt(T.okd[:], T.okn[:].indirect(T.offp[:]), T.dj[:], A.mult, ["okn", "offp", "dj"], ["okd"])
         unpack(2)
@@ -376,16 +394,19 @@ def rank_program(g, core, T, topo):
         scan(T.h0[:, ::-1], T.nok[:, ::-1], T.okd[:, ::-1], 0.0, A.mult, A.add, ["nok", "okd"], ["h0"])
         scan(T.lrow[:, 16:16 + C], T.nok[:], T.okd[:], T.h0[:, 0:1], A.mult, A.add, ["nok", "okd", "h0"], ["lrow"])
 
-        def to_list(row, tb, f, off):
-            turn(T[tb][:, 0:C], T[row][:, 16:16 + C], [row], [tb + "a"])
-            turn(T[tb][:, C:2 * C + 32], T[row][:], [row], [tb + "b"])
+        def pick(tb, f):
             tt(T[f][:], T[tb][:].indirect(T.offt[:]), T.plc[:], A.add, [tb + "a", tb + "b", "offt", "plc"], [f])
-            cp(T[off][:], T[f][:], [f], [off])
 
-        to_list("lrow", "ttl", "fl", "offl")
+        turn(T.ttl[:, 0:C], T.lrow[:, 16:16 + C], ["lrow"], ["ttla"])
+        turn(T.ttl[:, C:2 * C + 32], T.lrow[:], ["lrow"], ["ttlb"])
         scan(T.hrow[:, 15 + C:15:-1], T.nok[:, ::-1], T.okd[:, ::-1], T.lrow[:, 15 + C:16 + C], A.mult, A.add,
              ["nok", "okd", "lrow"], ["hrow"])
-        to_list("hrow", "tth", "fh", "offh")
+        pick("ttl", "fl")
+        turn(T.tth[:, 0:C], T.hrow[:, 16:16 + C], ["hrow"], ["ttha"])
+        cp(T.offl[:], T.fl[:], ["fl"], ["offl"])
+        turn(T.tth[:, C:2 * C + 32], T.hrow[:], ["hrow"], ["tthb"])
+        pick("tth", "fh")
+        cp(T.offh[:], T.fh[:], ["fh"], ["offh"])
         if t == R - 1:
             dma("pool", T.od[:, 0:C], T.lrow[0:128:16, 16:16 + C], ["lrow"], [])
             dma("pool", T.od[:, C:2 * C], T.hrow[0:128:16, 16:16 + C], ["hrow"], [])
@@ -397,7 +418,9 @@ def rank_program(g, core, T, topo):
                     planes + ["offl"], ["tl%d%d" % (h, b)])
                 tt(T.yt[:, 4 * h * H + b:4 * (h + 1) * H:4], T.p3[:, b, :].indirect(T.offh[:, 12 * h:12 * h + 11]),
                    T.tl[:, a:a + H], A.add, planes + ["offh", "tl%d%d" % (h, b)], ["yt%d%d" % (h, b)])
-            quant("qy", "sy", "yt", h * H, H, ["yt%d%d" % (h, b) for b in range(4)], ["qy%d" % h])
+                if (h, b) == (1, 0):
+                    quant("qy", "sy", "yt", 0, H, ["yt0%d" % k for k in range(4)], ["qy0"])
+        quant("qy", "sy", "yt", H, H, ["yt1%d" % k for k in range(4)], ["qy1"])
         for h in range(2):
             for b in range(4):
                 a = b * C + h * H
@@ -422,10 +445,11 @@ def rank_program(g, core, T, topo):
                 dma("sp", T.oc[:, 4 * h * H:4 * (h + 1) * H], u8(T[qn][:, h * H:(h + 1) * H]), [qn + str(h)], [])
 
     last = ["qx%d0" % R, "qx%d1" % R]
+    act(T.ysb[:, 0:H], T.psw[:, 0:H], ACT.Copy, ["psw0"], ["ysb0"])
+    dma("act", T.y[:, 0:H], T.ysb[:, 0:H], ["ysb0"], [])
     for k in range(4):
-        dma("pool" if k % 2 else "sp", T.osc[4 * k:4 * k + 4, :], T["sx%d" % R][32 * k:32 * k + 4, :], last, [])
-    for h in range(2):
-        act(T.ysb[:, h * H:(h + 1) * H], T.psw[:, 512 * h:512 * h + H], ACT.Copy, ["psw%d" % h], ["ysb%d" % h])
-        dma("act", T.y[:, h * H:(h + 1) * H], T.ysb[:, h * H:(h + 1) * H], ["ysb%d" % h], [])
+        dma("act" if k % 2 else "sp", T.osc[4 * k:4 * k + 4, :], T["sx%d" % R][32 * k:32 * k + 4, :], last, [])
+    cp(T.ysb[:, H:C], T.psw[:, 512:512 + H], ["psw1"], ["ysb1"])
+    dma("act", T.y[:, H:C], T.ysb[:, H:C], ["ysb1"], [])
     for sem, n in count.items():
         await_("pool", (sem, n, {}, "end"))

from concourse.mybir import dt, AluOpType, ActivationFunctionType

C, V, R = 352, 17, 3
STEP = [1, 2, 4]
H = C // 2
CH = C // 16
ND = 2 * V + 1
WIN = CH + 2 * V
CHUNKS = [[4, 7, 5, 6], [8, 8, 6]]
CMAX = 8
X0, NX, NC = 4, 7, 16
BIG = 1.0e29
PW = 400
F32, BF, I32, U16, QC, QS = "float32", "bfloat16", "int32", "uint16", "float8_e4m3fn_x4", "uint8"

SCRATCH = {"psf": ("psum", [128, 2048], F32), "psw": ("psum", [128, 2048], F32)}
for _d, _bufs in (
    (BF, dict(xin=[4 * C], ut=[512], vt=[512], ones=[128], ident=[128], ebig=[2048], zer=[512], nf=[2 * CH * ND],
              ko=[(CH + 32) * ND], rst=[CMAX * ND], kt=[CMAX * ND], tab=[48], t1=[32], zz=[768], dr3=[18, 32],
              dnat=[18 * CH], cmpn=[C], dj=[C], okn=[C], nok=[C], okd=[C], h0=[C], lrow=[C + 32], hrow=[C + 32],
              ttl=[2 * C + 32], tth=[2 * C + 32], p3=[4, PW], tl=[4 * C], yt=[4 * C], xt=[4 * C])),
    (F32, dict(spad=[16, 32], tsc=[512], gsc=[96], w3=[3, 32], dif=[2 * CH * ND], mn=[2 * CH * ND + 1], o1f=[CH],
               fl=[32], fh=[32], tr=[4 * C], ysb=[C], pf=[4], j16=[CH], jf=[CH], cnt=[32], ca=[32], cb=[32],
               c1=[CH], plc=[32], rep=[16 * NC], raw=[16 * NC], cc=[NC], cd=[NC])),
    (I32, dict(ig=[6], ig2=[6], pi=[4], ia=[32], ib=[32], ic=[32], ie=[NC])),
    (U16, dict(off1=[CH], off2=[CH], offl=[32], offh=[32], offg=[6], offz=[4], offp=[CH], offt=[2], offa=[NC],
               offb=[NC])),
    (QC, dict(qu=[128], qv=[128], qw=[512], qe=[512], qy=[C])),
    (QS, dict(su=[128], sv=[128], sw=[512], se=[512], sy=[C])),
):
    for _n, _s in _bufs.items():
        SCRATCH[_n] = ("sbuf", [128] + _s, _d)
for _t in range(R + 1):
    SCRATCH["qx%d" % _t] = ("sbuf", [128, C], QC)
    SCRATCH["sx%d" % _t] = ("sbuf", [128, C], QS)
for _t in range(R):
    SCRATCH["ql%d" % _t] = ("sbuf", [128, C], QC)
    SCRATCH["sl%d" % _t] = ("sbuf", [128, C], QS)
    SCRATCH["rq%d" % _t] = ("sbuf", [128, H], QC)
    SCRATCH["rs%d" % _t] = ("sbuf", [128, H], QS)
    SCRATCH["wo%d" % _t] = ("sbuf", [128, 3 * CH], F32)
    SCRATCH["wp%d" % _t] = ("sbuf", [128, WIN], F32)

SEMAPHORES = ["pe", "dve", "act", "pool", "sent", "sent0"] + ["dma%d" % i for i in range(24)]
for _t in range(R):
    SEMAPHORES += ["asc%d" % _t, "adir%d" % _t, "ahop%d" % _t, "rc%d" % _t, "rsc%d" % _t]

A = AluOpType
ACT = ActivationFunctionType


def helper_of(core, T, topo):
    r = T.rank_of(core)
    for c in topo.cores_of(core):
        if topo.die(c) != topo.die(core) and T.rank_of(c) is None and all(
                topo.may_write(c, T.cores[r ^ s]) for s in STEP):
            return c
    raise ValueError("no helper core")


def bits(engines):
    return sum(1 << e for e in engines)


def u8(view):
    return view.bitcast(dt.uint8)


def helper_program(g, core, rank, T, topo):
    total = 0
    for t in range(R):
        dst = T.cores[rank ^ STEP[t]]
        rid, pid = topo.addr(dst, core)
        m = topo.mask(core, dst)
        n = len(topo.engines(core, dst))
        hops = [("rsc", T["sl%d" % t][:, 0:H], T["rs%d" % t][:]),
                ("rc", u8(T["ql%d" % t][:, 0:H]), u8(T["rq%d" % t][:]))]
        for sem, out, in_ in (hops if t == 0 else hops[::-1]):
            g.wait_ge(T.sem["%s%d" % (sem, t)], n)
            g.remote_dma(out, in_, T.sem["ahop%d" % t], T.sem.sent, pid, rid, m)
        total += 2 * n
    g.wait_ge(T.sem.sent, total)


def rank_program(g, core, T, topo):
    rank = T.rank_of(core)
    if rank is None:
        for r, c in enumerate(T.cores):
            if helper_of(c, T, topo) == core:
                helper_program(g, core, r, T, topo)
        return

    Q = {"pe": g.tensor, "dve": g.vector, "act": g.scalar, "pool": g, "sp": g.sync}
    known = {e: {} for e in Q}
    count = {}
    writer, readers = {}, {}
    ndma = [0]

    def await_(e, ev):
        sem, n, snap, _ = ev
        if known[e].get(sem, 0) >= n:
            return
        Q[e].wait_ge(T.sem[sem], n)
        known[e][sem] = n
        for s, k in snap.items():
            if known[e].get(s, 0) < k:
                known[e][s] = k

    def deps(e, rd, wr):
        evs = []
        for k in rd:
            if k in writer:
                evs.append(writer[k])
            if k.startswith("ps"):
                evs += [x for x in readers.get(k, []) if x[3] != e]
        for k in wr:
            if k in writer:
                evs.append(writer[k])
            evs += readers.get(k, [])
        for ev in sorted(evs, key=lambda x: -x[1]):
            await_(e, ev)

    def note(ev, rd, wr):
        for k in rd:
            readers.setdefault(k, []).append(ev)
        for k in wr:
            writer[k] = ev
            readers[k] = []

    def op(e, fn, rd, wr):
        deps(e, rd, wr)
        count[e] = count.get(e, 0) + 1
        fn().then_inc(T.sem[e], 1)
        note((e, count[e], dict(known[e]), e), rd, wr)

    def dma(e, out, in_, rd, wr):
        deps(e, rd, wr)
        sem = "dma%d" % ndma[0]
        ndma[0] += 1
        count[sem] = 16
        Q[e].dma_start(out, in_).then_inc(T.sem[sem], 16)
        note((sem, 16, dict(known[e]), "dma"), rd, wr)

    def send(out, in_, dst, mask, rsem, rd, lsem="sent"):
        deps("pool", rd, [])
        rid, pid = topo.addr(dst, core)
        g.remote_dma(out, in_, T.sem[rsem], T.sem[lsem], pid, rid, mask)
        count[lsem] = count.get(lsem, 0) + bin(mask).count("1")

    def arrives(sem, n, keys):
        count[sem] = n
        for k in keys:
            writer[k] = (sem, n, {}, "far")

    v, s, pe = g.vector, g.scalar, g.tensor

    def vec(fn, rd, wr):
        op("dve", fn, rd, wr)

    def act(out, in_, f, rd, wr, **kw):
        op("act", lambda: s.activation(out, in_, f, **kw), rd, wr)

    def ts(out, in0, s1, s2, op0, op1, rd, wr):
        if op1 is None:
            vec(lambda: v.tensor_scalar(out, in0, s1, None, op0), rd, wr)
        else:
            vec(lambda: v.tensor_scalar(out, in0, s1, s2, op0, op1), rd, wr)

    def tt(out, in0, in1, o, rd, wr):
        vec(lambda: v.tensor_tensor(out, in0, in1, o), rd, wr)

    def cp(out, in_, rd, wr):
        vec(lambda: v.tensor_copy(out, in_), rd, wr)

    def turn(out, in_, rd, wr):
        vec(lambda: v.transpose(out, in_), rd, wr)

    def scan(out, d0, d1, init, op0, op1, rd, wr):
        vec(lambda: v.tensor_tensor_scan(out, d0, d1, init, op0, op1), rd, wr)

    def fill(ap, val, wr):
        vec(lambda: v.memset(ap, val), [], wr)

    def mm(ps, bank, lq, ls, l0, rq, rs, r0, n, rd):
        op("pe", lambda: pe.matmul_mx(T[ps][:, 512 * bank:512 * bank + n], T[lq][:, l0:l0 + 128], T[ls][:, l0:l0 + 128],
                                      T[rq][:, r0:r0 + n], T[rs][:, r0:r0 + n], True, True), rd, ["%s%d" % (ps, bank)])

    def quant(q, sc, src, c0, n, rd, wr):
        vec(lambda: v.quantize_mx(T[q][:, c0:c0 + n], T[sc][:, c0:c0 + n], T[src][:, 4 * c0:4 * (c0 + n)]), rd, wr)

    def iota(out, pat, base, cm, wr, small=False):
        if small:
            op("pool", lambda: g.iota(out, pat, base, cm, allow_small_or_imprecise_dtypes=True), [], wr)
        else:
            op("pool", lambda: g.iota(out, pat, base, cm), [], wr)

    helper = helper_of(core, T, topo)
    near = topo.engines(core, helper)
    far = topo.engines(core, T.cores[rank ^ STEP[0]])
    inner = [e for e in near if e not in far]
    nfar = len(far)

    dma("sp", T.xin[:, 0:4 * H], T.x[:, 0:4 * H], [], ["xin0"])
    dma("act", T.ut[:], T.u[:], [], ["ut"])
    dma("sp", T.xin[:, 4 * H:4 * C], T.x[:, 4 * H:4 * C], [], ["xin1"])
    fill(T.ones[:], 1.0, ["ones"])
    fill(T.zer[:], 0.0, ["zer"])
    fill(T.zz[:], 0.0, ["zz"])
    iota(T.ig[:], [[32, 3], [16, 2]], 32 * 15, 32, ["ig"])
    iota(T.pi[:, 0:1], [[0, 1]], 0, 1, ["pi0"])
    iota(T.j16[:], [[16, CH]], 0, 0, ["j16"], True)
    iota(T.cnt[:], [[1, 32]], 0, 0, ["cnt"], True)
    iota(T.kt[:], [[0, CMAX], [-1, ND]], ND, 0, ["kt"], True)
    iota(T.tab[:], [[-1, 48]], ND + 1, 0, ["tab"], True)
    op("pool", lambda: g.affine_select(T.ident[:], T.ones[:], [[-1, 128]], A.is_equal, 0.0, 0, 1), ["ones"], ["ident"])
    act(T.spad[:], T.zer[:], ACT.Copy, ["zer"], ["spad0", "spad1"])
    act(T.lrow[:], T.zer[:, 0:C + 32], ACT.Copy, ["zer"], ["lrow"])
    act(T.hrow[:], T.zer[:, 0:C + 32], ACT.Copy, ["zer"], ["hrow"])
    fill(T.mn[:, 0:1], 0.0, ["mnp"])
    fill(T.ko[:, 2 * CH * ND:(CH + 32) * ND], 0.0, ["kop"])
    ts(T.ig2[:], T.ig[:], 511, None, A.bitwise_and, None, ["ig"], ["ig2"])
    ts(T.pi[:, 1:2], T.pi[:, 0:1], 15, None, A.bitwise_and, None, ["pi0"], ["pi1"])
    ts(T.pi[:, 2:3], T.pi[:, 0:1], 4, 1, A.arith_shift_right, A.bitwise_and, ["pi0"], ["pi2"])
    cp(T.offg[:], T.ig2[:], ["ig2"], ["offg"])
    cp(T.pf[:, 0:1], T.pi[:, 1:2], ["pi1"], ["pf0"])
    cp(T.pf[:, 2:3], T.pi[:, 2:3], ["pi2"], ["pf2"])
    ts(T.pf[:, 1:2], T.pi[:, 1:2], float(CH), None, A.mult, None, ["pi1"], ["pf1"])
    ts(T.jf[:], T.j16[:], T.pf[:, 0:1], None, A.add, None, ["j16", "pf0"], ["jf"])
    ts(T.pf[:, 3:4], T.pi[:, 2:3], 16.0, None, A.mult, None, ["pi2"], ["pf3"])
    ts(T.cc[:], T.jf[:, 0:NC], -float(V), 1.0 / ND, A.add, A.mult, ["jf"], ["cc"])
    ts(T.c1[:], T.cnt[:, 0:CH], T.pf[:, 1:2], float(CH + V + 1), A.add, A.add, ["cnt", "pf1"], ["c1"])
    cp(T.ie[:], T.cc[:], ["cc"], ["ie"])
    ts(T.ia[:, 0:4], T.jf[:, 0:4], 30.0, None, A.add, None, ["jf"], ["ia"])
    ts(T.cd[:], T.ie[:], float(1 - ND), float(X0), A.mult, A.add, ["ie"], ["cd"])
    ts(T.offa[:], T.ie[:], float(CH + X0), None, A.add, None, ["ie"], ["offa"])
    tt(T.cc[:], T.cd[:], T.jf[:, 0:NC], A.add, ["cd", "jf"], ["cc"])
    ts(T.rst[:], T.kt[:], float(ND), BIG, A.is_equal, A.mult, ["kt"], ["rst"])
    cp(T.offb[:], T.cc[:], ["cc"], ["offb"])
    quant("qu", "su", "ut", 0, 128, ["ut"], ["qu"])

    def late_constants():
        for b in range(4):
            act(T.ebig[:, 512 * b:512 * (b + 1)], T.zer[:], ACT.Copy, ["zer"], ["e%d" % b])
        for b in range(4):
            act(T.ebig[:, 512 * b + b:512 * (b + 1):4], T.ident[:], ACT.Copy, ["ident"], ["e%d" % b])
        ts(T.ca[:, 0:CH], T.jf[:], -0.5 * (CH - 1), 1.0 / CH, A.add, A.mult, ["jf"], ["ca"])
        ts(T.ib[:, 0:4], T.ia[:, 0:4], 1, 15, A.arith_shift_right, A.bitwise_and, ["ia"], ["ib"])
        ts(T.ic[:, 0:4], T.ia[:, 0:4], 1, None, A.bitwise_and, None, ["ia"], ["ic"])
        cp(T.ia[:, 0:CH], T.ca[:, 0:CH], ["ca"], ["ia"])
        ts(T.ic[:, 4:8], T.ic[:, 0:4], 16.0, None, A.mult, None, ["ic"], ["ic4"])
        ts(T.cb[:, 0:CH], T.jf[:], 16.0, None, A.mult, None, ["jf"], ["cb"])
        ts(T.ca[:, 0:CH], T.ia[:, 0:CH], float(1 - C), None, A.mult, None, ["ia"], ["ca"])
        tt(T.ib[:, 4:8], T.ib[:, 0:4], T.ic[:, 4:8], A.add, ["ib", "ic4"], ["ib4"])
        tt(T.ca[:, 0:CH], T.ca[:, 0:CH], T.cb[:, 0:CH], A.add, ["ca", "cb"], ["ca"])
        cp(T.offz[:], T.ib[:, 4:8], ["ib4"], ["offz"])
        cp(T.offp[:], T.ca[:, 0:CH], ["ca"], ["offp"])
        ts(T.cb[:], T.cnt[:], 12.0, -1.0, A.is_ge, A.mult, ["cnt"], ["cb"])
        ts(T.ca[:, 0:2], T.jf[:, 0:2], 12.0, -1.0, A.is_ge, A.mult, ["jf"], ["ca"])
        tt(T.cb[:], T.cb[:], T.cnt[:], A.add, ["cb", "cnt"], ["cb"])
        tt(T.ca[:, 0:2], T.ca[:, 0:2], T.jf[:, 0:2], A.add, ["ca", "jf"], ["ca"])
        ts(T.cb[:], T.cb[:], 16.0, float(V), A.mult, A.add, ["cb"], ["cb"])
        ts(T.ca[:, 0:2], T.ca[:, 0:2], float(CH), 1.0, A.min, A.add, ["ca"], ["ca"])
        ts(T.plc[:], T.cb[:], T.pf[:, 0:1], None, A.add, None, ["cb", "pf0"], ["plc"])
        ts(T.ia[:, 0:2], T.ca[:, 0:2], T.pf[:, 2:3], None, A.subtract, None, ["ca", "pf2"], ["ia"])
        ts(T.ib[:, 0:2], T.ia[:, 0:2], 1, None, A.arith_shift_right, None, ["ia"], ["ib"])
        ts(T.ic[:, 0:2], T.ia[:, 0:2], 1, None, A.bitwise_and, None, ["ia"], ["ic"])
        ts(T.ca[:, 0:2], T.ib[:, 0:2], 32.0, T.pf[:, 3:4], A.mult, A.add, ["ib", "pf3"], ["ca"])
        ts(T.cb[:, 0:2], T.ic[:, 0:2], float(-C), float(C), A.mult, A.add, ["ic"], ["cb"])
        tt(T.ca[:, 0:2], T.ca[:, 0:2], T.cb[:, 0:2], A.add, ["ca", "cb"], ["ca"])
        cp(T.offt[:], T.ca[:, 0:2], ["ca"], ["offt"])
        for b in range(4):
            quant("qe", "se", "ebig", 128 * b, 128, ["e%d" % b], ["qe%d" % b])

    def first_half_out(t):
        send(u8(T["rq%d" % t][:]), u8(T["qx%d" % t][:, 0:H]), helper, bits(inner), "rc%d" % t, ["qx%d0" % t])
        send(T["rs%d" % t][:], T["sx%d" % t][:, 0:H], helper, bits(inner if t else far), "rsc%d" % t, ["qx%d0" % t])

    def side_product(t, h, q, sc):
        mm("psw", h, q, sc, 0, "qx%d" % t, "sx%d" % t, h * H, H, [q, "qx%d%d" % (t, h)])

    for h in range(2):
        quant("qx0", "sx0", "xin", h * H, H, ["xin%d" % h], ["qx0%d" % h])
        side_product(0, h, "qu", "su")
        if h == 0:
            first_half_out(0)

    for t in range(R):
        partner = T.cores[rank ^ STEP[t]]
        qx, sx, ql, sl = "qx%d" % t, "sx%d" % t, "ql%d" % t, "sl%d" % t
        kwo, kwp = "wo%d" % t, "wp%d" % t
        wo, wp = T[kwo], T[kwp]
        for h in range(2):
            act(T.spad[:, 8 * h:8 * h + 8, 0:CH], T.psw[:, 512 * h:512 * h + H], ACT.Copy,
                ["psw%d" % h], ["spad%d" % h])
            turn(T.tsc[:, 256 * h:256 * h + 256], T.spad[:, 8 * h:8 * h + 8, :], ["spad%d" % h], ["tsc%d" % h])
        cp(T.gsc[:], T.tsc[:].indirect(T.offg[:]), ["tsc0", "tsc1", "offg"], ["gsc"])
        turn(T.w3[:], T.gsc[:], ["gsc"], ["w3"])
        cp(wo[:], T.w3[:, :, 0:CH], ["w3"], [kwo])
        w0 = CH - V
        m = topo.mask(core, partner)
        send(wp[:], wo[:, w0:w0 + WIN], partner, m, "asc%d" % t, [kwo], "sent0" if t == 0 else "sent")
        send(u8(T[ql][:, H:C]), u8(T[qx][:, H:C]), partner, m, "adir%d" % t, [qx + "1"])
        send(T[sl][:, H:C], T[sx][:, H:C], partner, m, "adir%d" % t, [qx + "1"])
        arrives("asc%d" % t, nfar, [kwp])
        arrives("adir%d" % t, 2 * nfar, [ql + "1"])
        arrives("ahop%d" % t, 2 * nfar, [ql + "0"])
        if t == 0:
            await_("sp", ("sent0", count["sent0"], {}, "far"))
            dma("sp", u8(T.qw[:]), T.wc[:], [], ["qw"])
            dma("sp", T.sw[:], T.ws[:], [], ["sw"])
            dma("sp", T.vt[:], T.v[:], [], ["vt"])
            late_constants()
        if t == 1:
            quant("qv", "sv", "vt", 0, 128, ["vt"], ["qv"])
        for b in range(4):
            mm("psf", b, "qe", "se", 128 * b, qx, sx, 0, C, ["qe%d" % b, qx + "0", qx + "1"])
        for b in range(4):
            mm("psw", b, "qe", "se", 128 * b, ql, sl, 0, C, ["qe%d" % b, ql + "0", ql + "1"])

        steps = []
        for d in range(2):
            i0 = 0
            for n in CHUNKS[d]:
                steps.append((d, i0, n))
                i0 += n

        def span(c):
            d, i0, n = steps[c]
            return (d * CH + i0) * ND, (d * CH + i0 + n) * ND

        def least(c):
            d, i0, n = steps[c]
            a, e = span(c)
            scan(T.mn[:, 1 + a:1 + e], T.rst[:, 0:e - a], T.dif[:, a:e], 0.0, A.add, A.min,
                 ["rst"] + ["dif%d_%d" % (d, i) for i in range(i0, i0 + n)], ["mn%d" % c])

        act(T.rep[:], wo[:].indirect(T.offa[:]), ACT.Copy, [kwo, "offa"], ["rep"])
        tt(T.raw[:], wp[:].indirect(T.offb[:]), T.rep[:], A.subtract, [kwp, "offb", "rep"], ["raw"])
        for d in range(2):
            for i in range(CH):
                a = (d * CH + i) * ND
                if d == 0 and X0 <= i < X0 + NX:
                    if i == X0:
                        act(T.dif[:, a:a + NX * ND], T.raw[:, 0:NX * ND], ACT.Abs, ["raw"],
                            ["dif0_%d" % k for k in range(X0, X0 + NX)])
                    continue
                if d == 0:
                    win, mid = wp[:, i:i + ND], wo[:, CH + i:CH + i + 1]
                else:
                    win, mid = wo[:, w0 + i:w0 + i + ND], wp[:, V + i:V + i + 1]
                act(T.dif[:, a:a + ND], win, ACT.Abs, [kwo, kwp], ["dif%d_%d" % (d, i)], bias=mid, scale=-1.0)

        n0, nall = len(CHUNKS[0]), len(steps)
        k0 = ["ko%d" % c for c in range(n0)]
        k1 = ["ko%d" % c for c in range(n0, nall)]
        own = T.ko[:, ND - 1:CH * ND:ND]
        least(0)
        for c in range(nall):
            a, e = span(c)
            tt(T.nf[:, a:e], T.mn[:, 1 + a:1 + e], T.mn[:, a:e], A.is_equal,
               ["mn%d" % c, "mn%d" % (c - 1) if c else "mnp"], ["nf%d" % c])
            if c + 1 < nall:
                least(c + 1)
            if c == n0:
                cp(T.off2[:], own, k0, ["off2"])
                tt(T.o1f[:], T.c1[:], own, A.subtract, ["c1"] + k0, ["o1f"])
            scan(T.ko[:, a:e], T.nf[:, a:e], T.kt[:, 0:e - a], 0.0, A.mult, A.max, ["nf%d" % c, "kt"], ["ko%d" % c])
            if c == n0:
                cp(T.off1[:], T.o1f[:], ["o1f"], ["off1"])
        act(T.cmpn[:], T.tab[:].indirect(T.off2[:]), ACT.Copy, ["tab", "off2"], ["cmpn"])
        act(T.dj[:], T.cmpn[:].indirect(T.offp[:]), ACT.Identity, ["cmpn", "offp"], ["dj"], bias=-float(V + 1))

        def unpack(b):
            act(T.p3[:, b, V:V + C], T.psw[:, 512 * b:512 * b + C], ACT.Copy, ["psw%d" % b], ["p3_%d" % b], scale=0.5)

        unpack(0)
        unpack(1)
        turn(T.t1[:], T.ko[:, CH * ND + ND - 1:(CH + 32) * ND:ND], k1 + ["kop"], ["t1"])
        cp(T.zz[:, 0:768:16], T.t1[:].indirect(T.offz[:, 0:3]), ["t1", "offz"], ["zz"])
        for h in range(2):
            turn(T.dr3[:, 9 * h:9 * h + 9, :], T.zz[:, 288 * h:288 * h + 288], ["zz"], ["dr3%d" % h])
        for h in range(2):
            cp(T.dnat[:, 9 * CH * h:9 * CH * (h + 1)], T.dr3[:, 9 * h:9 * h + 9, 0:CH], ["dr3%d" % h], ["dnat%d" % h])
        tt(T.okn[:], T.dnat[:].indirect(T.off1[:]), T.cmpn[:], A.is_equal, ["dnat0", "dnat1", "off1", "cmpn"], ["okn"])
        act(T.nok[:], T.okn[:].indirect(T.offp[:]), ACT.Identity, ["okn", "offp"], ["nok"], bias=1.0, scale=-1.0)
        tt(T.okd[:], T.okn[:].indirect(T.offp[:]), T.dj[:], A.mult, ["okn", "offp", "dj"], ["okd"])
        unpack(2)
        unpack(3)
        planes = ["p3_%d" % b for b in range(4)]
        act(T.p3[:, :, 0:V], T.p3[:, :, C:C + V], ACT.Copy, planes, ["p3a"])
        act(T.p3[:, :, V + C:PW], T.p3[:, :, V:PW - C], ACT.Copy, planes, ["p3b"])
        planes += ["p3a", "p3b"]

        scan(T.h0[:, ::-1], T.nok[:, ::-1], T.okd[:, ::-1], 0.0, A.mult, A.add, ["nok", "okd"], ["h0"])
        scan(T.lrow[:, 16:16 + C], T.nok[:], T.okd[:], T.h0[:, 0:1], A.mult, A.add, ["nok", "okd", "h0"], ["lrow"])

        def pick(tb, f):
            tt(T[f][:], T[tb][:].indirect(T.offt[:]), T.plc[:], A.add, [tb + "a", tb + "b", "offt", "plc"], [f])

        turn(T.ttl[:, 0:C], T.lrow[:, 16:16 + C], ["lrow"], ["ttla"])
        turn(T.ttl[:, C:2 * C + 32], T.lrow[:], ["lrow"], ["ttlb"])
        scan(T.hrow[:, 15 + C:15:-1], T.nok[:, ::-1], T.okd[:, ::-1], T.lrow[:, 15 + C:16 + C], A.mult, A.add,
             ["nok", "okd", "lrow"], ["hrow"])
        pick("ttl", "fl")
        turn(T.tth[:, 0:C], T.hrow[:, 16:16 + C], ["hrow"], ["ttha"])
        cp(T.offl[:], T.fl[:], ["fl"], ["offl"])
        turn(T.tth[:, C:2 * C + 32], T.hrow[:], ["hrow"], ["tthb"])
        pick("tth", "fh")
        cp(T.offh[:], T.fh[:], ["fh"], ["offh"])
        if t == R - 1:
            dma("pool", T.od[:, 0:C], T.lrow[0:128:16, 16:16 + C], ["lrow"], [])
            dma("pool", T.od[:, C:2 * C], T.hrow[0:128:16, 16:16 + C], ["hrow"], [])

        for h in range(2):
            for b in range(4):
                a = b * C + h * H
                act(T.tl[:, a:a + H], T.p3[:, b, :].indirect(T.offl[:, 12 * h:12 * h + 11]), ACT.Copy,
                    planes + ["offl"], ["tl%d%d" % (h, b)])
                tt(T.yt[:, 4 * h * H + b:4 * (h + 1) * H:4], T.p3[:, b, :].indirect(T.offh[:, 12 * h:12 * h + 11]),
                   T.tl[:, a:a + H], A.add, planes + ["offh", "tl%d%d" % (h, b)], ["yt%d%d" % (h, b)])
                if (h, b) == (1, 0):
                    quant("qy", "sy", "yt", 0, H, ["yt0%d" % k for k in range(4)], ["qy0"])
        quant("qy", "sy", "yt", H, H, ["yt1%d" % k for k in range(4)], ["qy1"])
        for h in range(2):
            for b in range(4):
                a = b * C + h * H
                mm("psw", b, "qw", "sw", 128 * b, "qy", "sy", h * H, H, ["qw", "sw", "qy%d" % h])
                act(T.tr[:, a:a + H], T.psw[:, 512 * b:512 * b + H], ACT.Relu, ["psw%d" % b], ["tr%d%d" % (h, b)],
                    scale=0.03125)
        u = t + 1
        qn, sn = "qx%d" % u, "sx%d" % u
        for h in range(2):
            for b in range(4):
                a = b * C + h * H
                tt(T.xt[:, 4 * h * H + b:4 * (h + 1) * H:4], T.tr[:, a:a + H],
                   T.psf[:, 512 * b + h * H:512 * b + (h + 1) * H], A.add,
                   ["tr%d%d" % (h, b), "psf%d" % b], ["xt%d%d" % (h, b)])
            quant(qn, sn, "xt", h * H, H, ["xt%d%d" % (h, b) for b in range(4)], [qn + str(h)])
            if u < R:
                side_product(u, h, "qu", "su")
                if h == 0:
                    first_half_out(u)
            else:
                side_product(u, h, "qv", "sv")
                dma("sp", T.oc[:, 4 * h * H:4 * (h + 1) * H], u8(T[qn][:, h * H:(h + 1) * H]), [qn + str(h)], [])

    last = ["qx%d0" % R, "qx%d1" % R]
    act(T.ysb[:, 0:H], T.psw[:, 0:H], ACT.Copy, ["psw0"], ["ysb0"])
    dma("act", T.y[:, 0:H], T.ysb[:, 0:H], ["ysb0"], [])
    for k in range(4):
        dma("act" if k % 2 else "sp", T.osc[4 * k:4 * k + 4, :], T["sx%d" % R][32 * k:32 * k + 4, :], last, [])
    cp(T.ysb[:, H:C], T.psw[:, 512:512 + H], ["psw1"], ["ysb1"])
    dma("act", T.y[:, H:C], T.ysb[:, H:C], ["ysb1"], [])
    for sem, n in count.items():
        await_("pool", (sem, n, {}, "end"))
